import numpy as np, ml_dtypes
CORES = [10,34,74,98]
N = 4
import mx_ref
BF = ml_dtypes.bfloat16
def gentries(a):
    return np.ascontiguousarray(a.reshape(8, 16, -1).transpose(0, 2, 1)).reshape(8, -1)
def gtable(e):
    e = np.asarray(e); return np.ascontiguousarray(e.reshape(8, -1, 16).transpose(0, 2, 1)).reshape(128, -1).astype(np.int32)
def gcols(t, e):
    v = np.concatenate([t.reshape(8, 16, -1, 4), np.zeros((8, 16, 1, 4), BF)], axis=2)
    return np.ascontiguousarray(np.stack([v[g][:, e[g]] for g in range(8)])).reshape(128, -1)
def gpick(z, e):
    return np.concatenate([z[16 * g:16 * g + 16][:, e[g]] for g in range(8)])
def tile(rs):
    return np.stack(rs, axis=2).reshape(128, -1).astype(BF)
def pick(q, e):
    c = np.concatenate([q[0].reshape(128, -1, 4), np.zeros((128, 1, 4), np.uint8)], axis=1); s = np.concatenate([q[1], np.ones((16, 1), np.uint8)], axis=1)
    return (np.ascontiguousarray(c[:, e].reshape(128, -1)), np.ascontiguousarray(s[:, e]))
def join(*qs):
    return (np.concatenate([q[0] for q in qs], axis=1), np.concatenate([q[1] for q in qs], axis=1))
def put(q, e, v):
    c, s = q[0].reshape(128, -1, 4).copy(), q[1].copy(); c[:, e] = v[0].reshape(128, -1, 4); s[:, e] = v[1]
    return (c.reshape(128, -1), s)
def pk(c, s):
    return (np.ascontiguousarray(c), mx_ref.live(s))
def emit(q):
    return q[0], q[1]
def packed(v, rng):
    q = [mx_ref.quantize(np.ascontiguousarray(v[r])) for r in range(N)]
    return np.stack([a for a, b in q]), np.stack([mx_ref.plane(b, rng) for a, b in q])
def f(rng, *shape):
    return mx_ref.flush((rng.standard_normal(shape, dtype=np.float32) * np.exp2(rng.integers(-2, 3, shape[:-1] + (1,)))).astype(BF))
def wide(rng, *shape, cols=0):
    v = rng.standard_normal(shape, dtype=np.float32) * np.exp2(rng.integers(-12, 13, shape)).astype(np.float32)
    if cols: v *= np.repeat(np.exp2(rng.integers(-cols, cols + 1, shape[:-2] + (1, shape[-1] // 4))) * (rng.random(shape[:-2] + (1, shape[-1] // 4)) > 0.0625), 4, axis=-1).astype(np.float32)
    return mx_ref.flush(v.astype(BF))
C, R = 320, 3
def big(v):
    v = v.astype(np.float32)
    v[np.abs(v) < np.float32(2.0 ** -16)] = 0
    return v.astype(BF)
def numbers_of(rng):
    return {"x": big(f(rng, N, 128, 4 * C)), "u": np.array(f(rng, N, 128, 512)), "v": np.array(f(rng, N, 128, 512))}
def lookups(e):
    return {"ct": np.stack([gtable(e[r]) for r in range(N)])}
def any_lookups(rng):
    return rng.integers(0, 16, (N, 8, 256))
def layers(rng):
    return big(f(rng, N, 128, 2048)).reshape(N, 8, 16, 4, 8, 16, 4)
def weights(rng, w):
    c, p = packed(np.ascontiguousarray(w).reshape(N, 128, 2048), rng)
    return {"wc": c, "ws": p}
def signs(c):
    return ((c[:, :, None] >> np.arange(3, -1, -1)[:, None]) & 1) * 2.0 - 1.0
def single(d, k):
    u = d["u"].reshape(N, 128, 128, 4)
    for b in range(4):
        u[:, :, b::16] = 0
        for h in range(0, 128, 16): u[:, h + b, h + b, 0] = k
    return u
def setup_inputs(rng):
    return {**numbers_of(rng), **lookups(any_lookups(rng)), **weights(rng, layers(rng))}
def setup_inputs_near(rng):
    d = numbers_of(rng)
    x = d["x"].reshape(N, 8, 16, C, 4)
    o = rng.permutation(N) % 4
    k = np.where(o < 2, 2.0 ** -30, 1.0)
    u = single(d, k.astype(np.float32).astype(BF))
    x[:, :, :8] = 0
    for r in range(N):
        s = rng.integers(-1, 2, (8, 4, C)) * k[r]
        for g in rng.permutation(8)[:4]: s[g, :, rng.integers(C)] = 2.0 ** 29 * rng.choice([-1.0, 1.0], 4)
        two = o[r] in (0, 3)
        x[r, :, :4, :, 0] = (s * (1.125 if two else 1.0)).astype(np.float32).astype(BF)
        if two:
            x[r, :, 4:8, :, 0] = (-s).astype(np.float32).astype(BF)
            for h in range(0, 128, 16):
                for b in range(4):
                    u[r, h + b, h + b, 0] = 1.125 * k[r]
                    u[r, h + 4 + b, h + b, 0] = 1.25 * k[r]
    w = layers(rng)
    w[:, :, :8] = 0
    w[:, :, :, :, :, :8] = 0
    return {"x": x.reshape(N, 128, 4 * C), "u": u.reshape(N, 128, 512), "v": d["v"], **lookups(any_lookups(rng)), **weights(rng, w)}
def setup_inputs_late(rng):
    d = numbers_of(rng)
    x = d["x"].reshape(N, 8, 16, C, 4)
    c = (rng.permutation(N) % 2 * 2.0 - 1.0).astype(np.float32).astype(BF)
    x[:, :, 0] = c[:, None, None, None]
    u = d["u"].reshape(N, 128, 128, 4)
    for b in range(4):
        u[:, :, b::16] = 0
        for h in range(0, 128, 16): u[:, h, h + b, b] = 1
    return {"x": x.reshape(N, 128, 4 * C), "u": u.reshape(N, 128, 512), "v": d["v"], **lookups(any_lookups(rng)), **weights(rng, layers(rng))}
def setup_inputs_one(rng):
    d = numbers_of(rng)
    x = d["x"].reshape(N, 8, 16, C, 4)
    c, e, n = rng.integers(0, 16, (N, 8, C)), any_lookups(rng), np.arange(256)
    for r in rng.permutation(N)[:N // 2]:
        a = (rng.integers(C) - np.arange(C)) % C
        h = np.arange(8)[:, None] % 2
        c[r] = np.where(a < 256, np.where(h == 0, a // 16, a % 16), c[r])
        e[r] = np.where(h == 0, n // 16, n % 16)
        e[r, 7] = n // 16
    x[:, :, :8] = 0
    x[:, :, :4, :, 0] = signs(c).astype(np.float32).astype(BF)
    u = single(d, np.ones(N, np.float32).astype(BF))
    w = layers(rng)
    w[:, :, :, :, :, :8] = 0
    return {"x": x.reshape(N, 128, 4 * C), "u": u.reshape(N, 128, 512), "v": d["v"], **lookups(e), **weights(rng, w)}
def setup_inputs_ends(rng):
    d = numbers_of(rng)
    o = rng.permutation(N) % 4
    u = single(d, np.where(o == 1, 2.0 ** -30, 2.0 ** 30).astype(np.float32).astype(BF))
    x = 2.0 ** 30 * (0.75 + 0.1 * rng.random((N, 8, 16, C, 4))) * rng.choice([-1.0, 1.0], (N, 8, 1, C, 1))
    x[:, :, :8] = 0
    x[:, :, :4, :, 0] = signs(rng.integers(0, 16, (N, 8, C))) * 2.0 ** 30
    e = rng.integers(0, 2, (N, 8, 256)) * 15
    w = np.zeros((N, 128, 4, 128, 4), np.float32)
    i = np.arange(128)
    i = i[i % 16 >= 8]
    for r in range(N):
        if o[r] == 0:
            x[r] = 2.0 ** 30 * rng.choice([-1.0, 1.0], (1, 1, C, 1))
            for b in range(4): u[r][:, b::16] = (2.0 ** 30 * rng.choice([-1.0, 1.0], (1, 8, 1)) * np.ones((128, 1, 4))).astype(np.float32).astype(BF)
            e[r] = 15
        if o[r] == 1:
            x[r, :, :4] *= 2.0 ** -60
            x[r, :, 8:] = 2.0 ** -30 * rng.choice([-1.0, 1.0], (8, 8, C, 4))
            e[r] = 0
        if o[r] == 2: x[r, :, :8] = 0
        if o[r] == 3: e[r] = rng.integers(0, 2, (8, 1)) * 15
        if o[r] >= 2:
            for b in range(4): w[r, i, b, i, b] = rng.choice([-1.0, 1.0], len(i))
    d["v"] = (np.where(d["v"] < 0, -1.0, 1.0) * np.where(rng.permutation(N) % 2, 2.0 ** -30, 2.0 ** 30)[:, None, None]).astype(np.float32).astype(BF)
    return {"x": x.astype(np.float32).reshape(N, 128, 4 * C).astype(BF), "u": u.reshape(N, 128, 512), "v": d["v"], **lookups(e), **weights(rng, w.astype(BF))}
def setup_inputs_spread(rng):
    d = setup_inputs(rng)
    d["x"] = big(wide(rng, N, 128, 4 * C, cols=6))
    return d
def check_inputs(d):
    b = []
    for k in ("x", "u", "v"):
        a = np.abs(d[k].astype(np.float32))
        if not (np.isfinite(a).all() and ((a == 0) | (a >= 2.0 ** -30) & (a <= 2.0 ** 30)).all()): b.append("a value of " + k)
    if not ((d["ct"] >= 0) & (d["ct"] < 16)).all(): b.append("an entry of ct")
    none, least, most = [emit(mx_ref.quantize(np.full((128, 16), k, np.float32).astype(BF)))[1][0, 0] for k in (0.0, 2.0 ** -30, 2.0 ** 30)]
    for r in range(N):
        if ((d["wc"][r] == 0x7F) | (d["wc"][r] == 0xFF)).any(): b.append("wc: a code that is no number")
        s = mx_ref.live(d["ws"][r])
        if ((s != none) & ((s < least) | (s > most))).any(): b.append("ws: a scale out of range")
    return b
def reference(x, u, v, ct, wc, ws):
    qu = [mx_ref.quantize(u[r]) for r in range(N)]
    lay = [pk(wc[r], ws[r]) for r in range(N)]
    now = [x[r] for r in range(N)]
    k = [gentries(ct[r]) for r in range(N)]
    for t in range(R):
        place, z = [], []
        for r in range(N):
            s = (mx_ref.matmul(qu[r], mx_ref.quantize(now[r])) > 0).astype(np.int64)
            c = 8 * s[::16] + 4 * s[1::16] + 2 * s[2::16] + s[3::16]
            a = np.zeros((8, C), np.int64)
            a[:4] = 16 * c[::2] + c[1::2]
            a[4] = 16 * k[r][0][a[0]] + k[r][1][a[1]]
            a[5] = 16 * k[r][2][a[2]] + k[r][3][a[3]]
            a[6] = 16 * k[r][4][a[4]] + k[r][5][a[5]]
            a[7] = 16 * k[r][6][a[6]] + k[r][7][16 * c[7] + c[0]]
            place.append((a + np.arange(C)) % C)
            z.append(mx_ref.quantize(gcols(now[r], place[r])))
        made = []
        for r in range(N):
            q, e = z[(r - 1 - t) % N], place[r][[1, 0, 3, 2, 5, 4, 7, 6]]
            made.append(tile([gpick(mx_ref.matmul(pick(lay[r], np.arange(128 * b, 128 * b + 128)), q) * np.float32(0.03125), e) + now[r][:, b::4].astype(np.float32) for b in range(4)]))
        now = made
    y, lo = np.zeros((N, 128, C), np.float32), np.zeros((N, 8, C), np.float32)
    oc, osc = np.zeros((N, 128, 4 * C), np.uint8), np.zeros((N, 16, C), np.uint8)
    for r in range(N):
        q = mx_ref.quantize(now[r])
        y[r] = mx_ref.matmul(mx_ref.quantize(v[r]), q)
        lo[r] = place[r]
        oc[r], osc[r] = emit(q)
    return {"y": y, "lo": lo, "oc": oc, "osc": osc}

@@ -1,0 +1,386 @@
+from concourse.mybir import dt, AluOpType, ActivationFunctionType
+
+C = 320
+R = 3
+EXT = 256
+WIN = (0, 64, 192)
+TO = 72
+F32, BF, I32, U16 = "float32", "bfloat16", "int32", "uint16"
+MXC, MXS = "float8_e4m3fn_x4", "uint8"
+
+SCRATCH = {}
+
+
+def _sb(name, cols, dtype):
+    SCRATCH[name] = ("sbuf", [128, cols], dtype)
+
+
+for _t in range(R):
+    _sb("x%d" % _t, 4 * (C + EXT), BF)
+    _sb("qz%d" % _t, C, MXC)
+    _sb("sz%d" % _t, C, MXS)
+    _sb("lq%d" % _t, C, MXC)
+    _sb("ls%d" % _t, C, MXS)
+_sb("x%d" % R, 4 * C, BF)
+for _n, _c, _d in (
+        ("ub", 512, BF), ("vb", 512, BF), ("uq", 128, MXC), ("us", 128, MXS), ("uq2", 128, MXC), ("us2", 128, MXS),
+        ("vq", 128, MXC), ("vs", 128, MXS), ("wq", 512, MXC), ("wsc", 512, MXS), ("qx", C, MXC), ("sx", C, MXS),
+        ("z", 4 * C, BF), ("h", 4 * C, F32), ("yb", C, F32), ("lof", C, F32),
+        ("cta", 32, I32), ("ctb", 128, F32), ("cto", 128, U16), ("tab", 2048, BF),
+        ("pint", 2, I32), ("pi2", 4, I32), ("pf", 4, F32), ("kcol", 2, F32), ("uri", 8, I32), ("ur2", 8, I32), ("url", 8, U16),
+        ("n16", 192, BF), ("diag", 192, BF), ("m16", 48, BF), ("io32", 32, BF), ("io320", C, F32), ("zz", 192, BF),
+        ("fl", 96, BF), ("flm", 96, BF), ("flw", 96, BF), ("dwr", 192, BF), ("lst", 10, U16), ("ul", 8, U16),
+        ("fm2", 80, BF), ("fw2", 80, BF),
+        ("bt", 20, F32), ("ht", 20, F32), ("f1", 20, F32), ("f2", 20, F32), ("f3", 20, F32), ("f4", 20, F32),
+        ("ji", 80, F32), ("j4", 80, F32), ("hd0", 150, F32), ("thr", 50, F32), ("d1t", 192, BF), ("d03", 96, BF),
+        ("sg", 150, F32), ("sc0", 150, F32), ("off1", 16, U16), ("g1", 192, BF), ("sc1", 192, BF), ("off2", 6, U16),
+        ("g2", 96, BF), ("sc2", 96, BF), ("off3", 4, U16), ("g3", 96, BF), ("sc3", 96, BF),
+        ("la", 16, F32), ("dd", TO + 32, F32), ("at", 64, F32), ("x4", 80, F32), ("offz", 80, U16),
+        ("md", 20, F32), ("lp", 32, F32), ("lt", 64, F32), ("lsw", 32, F32), ("offg", 20, U16), ("offl", 20, U16)):
+    _sb(_n, _c, _d)
+SCRATCH["pss"] = ("psum", [128, 3 * 512], F32)
+SCRATCH["psh"] = ("psum", [128, 5 * 512], F32)
+
+RING = {"v": 44, "s": 32, "p": 16, "g": 24}
+NDMA = 20
+SEMAPHORES = ([q + str(k) for q in RING for k in range(RING[q])] + ["d%d" % k for k in range(NDMA)]
+              + ["arr%d" % t for t in range(R)] + ["sent"])
+
+
+def A(name, c0=None, c1=None, st=1, p0=0, p1=128, ps=1):
+    if c0 is None:
+        c0, c1 = 0, SCRATCH[name][1][1]
+    return (name, p0, p1, ps, c0, c1, st)
+
+
+def Qd(name, q, c0, c1, st=1):
+    return A(name, c0, c1, st, 32 * q, 32 * q + 32)
+
+
+def _foot(a):
+    name, p0, p1, ps, c0, c1, st = a
+    if name not in SCRATCH:
+        return None
+    if SCRATCH[name][0] == "psum":
+        return (name, 0, 128, frozenset(range(c0 // 512, (c1 - 1) // 512 + 1)), True)
+    return (name, p0, p1, frozenset(range(c0, c1, st)), False)
+
+
+def _meet(a, b):
+    return a[0] == b[0] and a[1] < b[2] and b[1] < a[2] and not a[3].isdisjoint(b[3])
+
+
+def rank_program(g, core, T, topo):
+    rank = T.rank_of(core)
+    if rank is None:
+        return
+    n = len(T.cores)
+    ops = []
+    eng = {"v": g.vector, "s": g.scalar, "p": g.tensor, "g": g, "y": g.sync}
+    add, mult, sub = AluOpType.add, AluOpType.mult, AluOpType.subtract
+    COPY, IDENT = ActivationFunctionType.Copy, ActivationFunctionType.Identity
+
+    def ap(a):
+        if not isinstance(a, tuple):
+            return a
+        if a[0] == "ind":
+            return ap(a[1]).indirect(ap(a[2]))
+        if a[0] == "indw":
+            return ap(a[1]).bitcast(dt.uint32).indirect(ap(a[2]))
+        if a[0] == "w":
+            return ap(a[1]).bitcast(dt.uint32)
+        if a[0] == "b":
+            return ap(a[1]).bitcast(dt.uint8)
+        name, p0, p1, ps, c0, c1, st = a
+        return T[name][slice(p0, p1, ps) if ps > 1 else slice(p0, p1), slice(c0, c1, st) if st > 1 else slice(c0, c1)]
+
+    def feet(args):
+        out = []
+        for a in args:
+            if isinstance(a, tuple):
+                if a[0] in ("ind", "indw", "w", "b"):
+                    out += feet(a[1:])
+                elif _foot(a) is not None:
+                    out.append(_foot(a))
+        return out
+
+    def op(q, call, outs, ins, kind="c", **more):
+        w, r = feet(outs), feet(ins)
+        w += [f for f in r if f[4]]
+        ops.append(dict(q=q, call=call, w=w, r=r, kind=kind, **more))
+
+    def ind(win, off):
+        return ("ind", win, off)
+
+    def copy(o, i):
+        op("v", lambda: g.vector.tensor_copy(ap(o), ap(i)), [o], [i])
+
+    def tt(o, a, b, f):
+        op("v", lambda: g.vector.tensor_tensor(ap(o), ap(a), ap(b), f), [o], [a, b])
+
+    def ts(o, a, s1, f1, s2=None, f2=None):
+        if f2 is None:
+            op("v", lambda: g.vector.tensor_scalar(ap(o), ap(a), ap(s1), None, f1), [o], [a, s1])
+        else:
+            op("v", lambda: g.vector.tensor_scalar(ap(o), ap(a), ap(s1), ap(s2), f1, f2), [o], [a, s1, s2])
+
+    def scan(o, d0, d1):
+        op("v", lambda: g.vector.tensor_tensor_scan(ap(o), ap(d0), ap(d1), 0.0, mult, add), [o], [d0, d1])
+
+    def fill(o, c):
+        op("v", lambda: g.vector.memset(ap(o), c), [o], [])
+
+    def turn(o, i):
+        op("v", lambda: g.vector.transpose(ap(o), ap(i)), [o], [i])
+
+    def quant(q, s, i):
+        op("v", lambda: g.vector.quantize_mx(ap(q), ap(s), ap(i)), [q, s], [i])
+
+    def act(o, i, scale=None, bias=None):
+        if bias is not None:
+            op("s", lambda: g.scalar.activation(ap(o), ap(i), IDENT, bias=ap(bias), scale=1.0 if scale is None else scale), [o], [i, bias])
+        elif scale is not None:
+            op("s", lambda: g.scalar.activation(ap(o), ap(i), COPY, scale=scale), [o], [i])
+        else:
+            op("s", lambda: g.scalar.activation(ap(o), ap(i), COPY), [o], [i])
+
+    def mm(o, lq, ls, rq, rs):
+        op("p", lambda: g.tensor.matmul_mx(ap(o), ap(lq), ap(ls), ap(rq), ap(rs), True, True), [o], [lq, ls, rq, rs])
+
+    def iota(o, pattern, base=0, cm=0):
+        if SCRATCH[o[0]][2] == I32:
+            op("g", lambda: g.iota(ap(o), pattern, base, cm), [o], [])
+        else:
+            op("g", lambda: g.iota(ap(o), pattern, base, cm, allow_small_or_imprecise_dtypes=True), [o], [])
+
+    def dma(q, o, i, last=False):
+        op(q, lambda: eng[q].dma_start(ap(o), ap(i)), [o], [i], kind="dma", last=last)
+
+    def send(t, pairs):
+        dst = T.cores[(rank + 1 + t) % n]
+        rid, pid, _ = topo.addr(dst)
+        mask = topo.mask(core, dst)
+        for o, i in pairs:
+            op("g", lambda o=o, i=i: g.remote_dma(ap(o), ap(i), T.sem["arr%d" % t], T.sem.sent, pid, rid, mask), [], [i],
+               kind="send", count=len(topo.engines(core, dst)))
+        src = T.cores[(rank - 1 - t) % n]
+        op("none", None, [o for o, i in pairs], [], kind="land", sem="arr%d" % t, val=len(pairs) * len(topo.engines(src, core)))
+
+    dma("y", A("cta", 0, 16), A("ct", 0, 16))
+    dma("s", A("cta", 16, 32, p0=0, p1=112), A("ct", 0, 16, p0=16, p1=128))
+    dma("y", A("cta", 16, 32, p0=112, p1=128), A("ct", 0, 16, p0=0, p1=16))
+    dma("s", A("ub"), A("u", 0, 512))
+    dma("y", A("x0", 0, 4 * C), A("x", 0, 4 * C))
+    dma("y", A("x0", 4 * C, 4 * (C + EXT)), A("x", 0, 4 * EXT))
+
+    def const(o, c):
+        act(o, A("zz", 0, len(range(o[4], o[5], o[6]))), bias=float(c))
+
+    icol, gcol, ecol = A("pf", 0, 1), A("pf", 1, 2), A("pf", 2, 3)
+    fill(A("fl"), 0.0)
+    fill(A("zz"), 0.0)
+    iota(A("pint", 0, 1), [[0, 1]], 0, 1)
+    iota(A("uri"), [[16, 8]], 143, -1)
+    iota(A("fl", 32, 72), [[32, 4], [16, 2], [1, 5]])
+    iota(A("fl", 72, 82), [[-112, 2], [1, 5]], 112)
+    iota(A("fl", 0, 12), [[50, 3], [10, 4]], 8)
+    iota(A("fl", 12, 15), [[50, 3]], 48)
+    iota(A("fl", 16, 28), [[20, 2], [50, 3], [10, 2]], 8)
+    iota(A("bt", 0, 8), [[3, 4], [0, 2]], TO)
+    iota(A("bt", 8, 12), [[3, 2], [0, 2]], TO + 7)
+    iota(A("bt", 12, 20), [[3, 4], [0, 2]], TO + 2)
+    iota(A("ht"), [[0, 10], [1, 2]])
+    iota(A("io32"), [[1, 32]], -16)
+    iota(A("ji"), [[1, 4], [64, 20]], 0, 4)
+    fill(A("dwr"), 1.0)
+    fill(A("ul"), 0)
+    ts(A("pi2", 0, 1), A("pint", 0, 1), 15, AluOpType.bitwise_and)
+    fill(A("dwr", 0, 192, 16), 0.0)
+    ts(A("pi2", 1, 2), A("pint", 0, 1), 4, AluOpType.arith_shift_right)
+    ts(A("pi2", 2, 3), A("pint", 0, 1), 4, AluOpType.arith_shift_right, 1, AluOpType.bitwise_and)
+    scan(A("n16"), A("dwr"), A("dwr"))
+    copy(A("pf", 0, 3), A("pi2", 0, 3))
+    ts(A("ur2"), A("uri"), 112, AluOpType.bitwise_and)
+    ts(A("diag"), A("n16"), icol, AluOpType.is_equal)
+    ts(A("url"), A("ur2"), icol, add)
+    fill(A("thr"), 0.0)
+    fill(A("dd"), 0.0)
+    fill(A("thr", 4, 50, 10), 1e29)
+    fill(A("thr", 9, 50, 10), -1e29)
+    fill(A("lp"), 0.0)
+    tt(A("flm"), A("fl"), A("diag", 0, 96), mult)
+    scan(A("flw"), A("dwr", 0, 96), A("flm"))
+    copy(A("ul", 0, 4), A("flw", 47, 96, 16))
+    copy(A("lst", 6, 10, 2), A("flw", 15, 32, 16))
+    const(A("hd0"), 2)
+    const(A("d1t"), 1)
+    const(A("d03"), 1)
+    const(A("hd0", 4, 150, 10), 1)
+    const(A("hd0", 9, 150, 10), 0)
+    for k, slot in ((0, 0), (2, 2), (3, 3), (4, 7)):
+        const(A("hd0", 10 * k, 150, 50), 2 * slot)
+    const(A("d1t", 0, 192, 32), 0)
+    const(A("d1t", 16, 192, 32), 16)
+    const(A("d03", 0, 96, 32), 0)
+    act(A("kcol", 0, 1, p0=0, p1=64), A("pf", 1, 2, p0=0, p1=64), scale=-1088.0)
+    act(Qd("kcol", 3, 0, 1), Qd("pf", 3, 1, 2), scale=-64.0)
+    act(Qd("kcol", 2, 0, 1), Qd("pf", 2, 2, 3), scale=-1088.0, bias=768.0)
+    act(A("m16"), A("diag", 0, 48), scale=16.0)
+    dma("g", ("b", A("wq")), A("wc", 0, 2048))
+    dma("g", A("wsc"), A("ws", 0, 512))
+    dma("g", A("vb"), A("v", 0, 512))
+
+    ts(A("f1"), A("ht"), ecol, AluOpType.is_equal)
+    ts(A("f2"), A("bt"), ecol, add, float(-2 * TO), add)
+    tt(A("f3"), A("f1"), A("f2"), mult)
+    tt(A("f4"), A("f3"), A("bt"), add)
+    for e in range(4):
+        tt(A("fm2", 20 * e, 20 * e + 20), A("f4"), A("diag", 20 * e, 20 * e + 20), mult)
+    scan(A("fw2"), A("dwr", 0, 80), A("fm2"))
+    copy(A("lst", 0, 5), A("fw2", 15, 80, 16))
+    act(A("j4"), A("ji"), bias=A("kcol", 0, 1))
+
+    copy(A("ctb", 0, 32), A("cta"))
+    for q in range(4):
+        if q < 2:
+            copy(Qd("ctb", q, 32, 64), Qd("cta", q + 1, 0, 32))
+        else:
+            act(Qd("ctb", q, 32, 64), Qd("ctb", (q + 1) % 4, 0, 32))
+    copy(A("ctb", 64, 128, p0=0, p1=64), A("ctb", 0, 64, p0=64, p1=128))
+    act(A("ctb", 64, 128, p0=64, p1=128), A("ctb", 0, 64, p0=0, p1=64))
+    copy(A("cto"), ind(A("ctb"), A("url")))
+    quant(A("uq"), A("us"), A("ub"))
+    act(A("tab", 0, 256), ind(A("io32", 0, 16), A("cto", 0, 16)))
+    act(A("tab", 256, 1024), ind(A("io32", 16, 32), A("cto", 16, 64)))
+    op("v", lambda: g.vector.tensor_copy(ap(("w", A("uq2"))), ap(("indw", A("uq"), A("ul")))), [A("uq2")], [A("uq"), A("ul")])
+    copy(A("us2"), ind(A("us"), A("ul")))
+    act(A("tab", 1024, 1536), ind(A("io32", 16, 32), A("cto", 64, 96)))
+
+    for t in range(R):
+        X, XN = "x%d" % t, "x%d" % (t + 1)
+        quant(A("qx", 0, WIN[2]), A("sx", 0, WIN[2]), A(X, 0, 4 * WIN[2]))
+        quant(A("qx", WIN[2], C), A("sx", WIN[2], C), A(X, 4 * WIN[2], 4 * C))
+        for m in range(3):
+            mm(A("pss", 512 * m, 512 * m + 128), A("qx", WIN[m], WIN[m] + 128), A("sx", WIN[m], WIN[m] + 128), A("uq2"), A("us2"))
+        for m in range(3):
+            tt(A("sg", 50 * m, 50 * m + 50), A("pss", 512 * m, 512 * m + 50), A("thr"), AluOpType.is_gt)
+        scan(A("sc0"), A("hd0"), A("sg"))
+        copy(A("off1"), ind(A("sc0"), A("lst", 6, 7)))
+        if t == 0:
+            copy(A("tab", 1536, 2048), ind(A("io32", 16, 32), A("cto", 96, 128)))
+        act(A("la"), ind(A("sc0"), A("lst", 8, 9)), scale=4.0)
+        for a in range(2):
+            for q in range(4):
+                act(Qd("dd", a, 6 * q, 6 * q + 6), Qd("la", q, 6 * a, 6 * a + 6))
+        tt(A("g1"), ind(A("tab", 0, 1024), A("off1", 0, 12)), A("diag"), mult)
+        scan(A("sc1"), A("d1t"), A("g1"))
+        ts(A("off2"), A("sc1", 31, 192, 32), 256.0, add)
+        for q in range(4):
+            act(Qd("dd", 2, 6 * q, 6 * q + 6), Qd("sc1", q, 31, 192, 32), scale=4.0)
+        tt(A("g2"), ind(A("tab", 1024, 1536), A("off2")), A("diag", 0, 96), mult)
+        tt(A("g3", 1, 96, 2), ind(A("tab"), A("off1", 12, 15)), A("diag", 0, 48), mult)
+        scan(A("sc2"), A("d1t", 0, 96), A("g2"))
+        copy(A("off3", 0, 3), A("sc2", 31, 96, 32))
+        for q in range(4):
+            act(Qd("dd", 3, 6 * q, 6 * q + 6, 2), Qd("sc2", q, 31, 96, 32), scale=4.0)
+        tt(A("g3", 0, 96, 2), ind(A("tab", 1536, 1792), A("off3", 0, 3)), A("m16"), mult)
+        scan(A("sc3"), A("d03"), A("g3"))
+        for q in range(2):
+            ts(Qd("dd", 3, 6 * q + 1, 6 * q + 6, 2), Qd("sc3", q, 31, 96, 32), 4.0, mult)
+        for q in range(2, 4):
+            act(Qd("dd", 3, 6 * q + 1, 6 * q + 6, 2), Qd("sc3", q, 31, 96, 32), scale=4.0)
+        turn(A("at", 0, 32), A("dd", 0, 64, 2))
+        turn(A("at", 32, 64), A("dd", 1, 65, 2))
+        turn(A("dd", TO, TO + 32), A("at", 16, 48))
+        tt(A("x4"), ind(A("dd"), A("lst", 0, 5)), A("j4"), add)
+        copy(A("offz"), A("x4"))
+        for e in range(2):
+            act(A("z", e, 4 * C, 4), ind(A(X), A("offz", 20 * e, 20 * e + 20)))
+        for e in range(2, 4):
+            copy(A("z", e, 4 * C, 4), ind(A(X), A("offz", 20 * e, 20 * e + 20)))
+        qz, sz, lq, ls = "qz%d" % t, "sz%d" % t, "lq%d" % t, "ls%d" % t
+        quant(A(qz), A(sz), A("z"))
+        send(t, [(("b", A(lq)), ("b", A(qz))), (A(ls), A(sz))])
+        ts(A("md"), A("x4", 0, 20), float(4 * C), AluOpType.is_ge, float(-4 * C), mult)
+        tt(A("lp", 0, 20), A("x4", 0, 20), A("md"), add)
+        turn(A("lt", 0, 32), A("lp"))
+        turn(A("lt", 32, 64), A("lp"))
+        turn(A("lsw"), A("lt", 16, 48))
+        ts(A("offg"), A("lsw", 0, 20), 0.25, mult)
+        if t == 0:
+            quant(A("vq"), A("vs"), A("vb"))
+            iota(A("io320"), [[1, C]])
+        if t == R - 1:
+            ts(A("offl"), A("lp", 0, 20), 0.25, mult)
+            act(A("lof"), ind(A("io320"), A("offl")))
+            dma("y", A("lo", 0, C, p0=0, p1=8), A("lof", 0, C, ps=16), last=True)
+        hc = C // 2
+        mm(A("psh", 0, hc), A("wq", 0, 128), A("wsc", 0, 128), A(lq, 0, hc), A(ls, 0, hc))
+        mm(A("psh", 2048, 2048 + hc), A("wq", 0, 128), A("wsc", 0, 128), A(lq, hc, C), A(ls, hc, C))
+        for b in range(1, 4):
+            mm(A("psh", 512 * b, 512 * b + C), A("wq", 128 * b, 128 * b + 128), A("wsc", 128 * b, 128 * b + 128), A(lq), A(ls))
+        act(A("h", 0, hc), A("psh", 0, hc), scale=0.03125)
+        ts(A("h", hc, C), A("psh", 2048, 2048 + hc), 0.03125, mult)
+        for b in range(1, 4):
+            act(A("h", C * b, C * b + C), A("psh", 512 * b, 512 * b + C), scale=0.03125)
+        for b in range(4):
+            tt(A(XN, b, 4 * C, 4), ind(A("h", C * b, C * b + C), A("offg")), A(X, b, 4 * C, 4), add)
+        if t < R - 1:
+            for b in range(4):
+                act(A(XN, 4 * C + b, 4 * (C + EXT), 4), A(XN, b, 4 * EXT, 4))
+
+    cut = WIN[2]
+    quant(A("qx", 0, cut), A("sx", 0, cut), A("x%d" % R, 0, 4 * cut))
+    quant(A("qx", cut, C), A("sx", cut, C), A("x%d" % R, 4 * cut, 4 * C))
+    mm(A("pss", 0, cut), A("vq"), A("vs"), A("qx", 0, cut), A("sx", 0, cut))
+    mm(A("pss", 512, 512 + C - cut), A("vq"), A("vs"), A("qx", cut, C), A("sx", cut, C))
+    dma("y", A("oc", 0, 4 * C), ("b", A("qx")), last=True)
+    for k in range(4):
+        dma("s" if k < 3 else "g", A("osc", 0, C, p0=4 * k, p1=4 * k + 4), A("sx", 0, C, p0=32 * k, p1=32 * k + 4), last=True)
+    copy(A("yb", 0, cut), A("pss", 0, cut))
+    copy(A("yb", cut, C), A("pss", 512, 512 + C - cut))
+    dma("y", A("y", 0, C), A("yb"), last=True)
+
+    known = {}
+    for k, o in enumerate(ops):
+        o["waits"] = []
+        seen = known.setdefault(o["q"], set())
+        if o["kind"] != "land":
+            for j in range(k - 1, -1, -1):
+                e = ops[j]
+                if j in seen or (o["q"] == "p" and e["q"] == "p"):
+                    continue
+                if (any(_meet(a, b) for a in o["r"] + o["w"] for b in e["w"]) or any(_meet(a, b) for a in o["w"] for b in e["r"])):
+                    o["waits"].append(j)
+                    e["need"] = True
+                    seen.add(j)
+                    seen.update(e["seen"])
+        o["seen"] = set(seen)
+    level, turnq, nd = {}, {}, 0
+    for o in ops:
+        if o["kind"] == "dma":
+            o["sem"], o["val"] = "d%d" % nd, 16
+            nd += 1
+        elif o["kind"] == "c" and o.get("need"):
+            k = turnq.get(o["q"], 0)
+            turnq[o["q"]] = k + 1
+            o["sem"] = o["q"] + str(k % RING[o["q"]])
+            level[o["sem"]] = level.get(o["sem"], 0) + 1
+            o["val"] = level[o["sem"]]
+    sent = 0
+    for o in ops:
+        if o["kind"] == "land":
+            continue
+        for j in o["waits"]:
+            eng[o["q"]].wait_ge(T.sem[ops[j]["sem"]], ops[j]["val"])
+        ins = o["call"]()
+        if o["kind"] == "send":
+            sent += o["count"]
+        elif o["kind"] == "dma":
+            ins.then_inc(T.sem[o["sem"]], 16)
+        elif o.get("need"):
+            ins.then_inc(T.sem[o["sem"]], 1)
+    g.wait_ge(T.sem.sent, sent)
+    for o in ops:
+        if o["kind"] == "dma" and o["last"]:
+            eng[o["q"]].wait_ge(T.sem[o["sem"]], 16)

@@ -26,7 +26,7 @@ for _n, _c, _d in (
         ("ub", 512, BF), ("vb", 512, BF), ("uq", 128, MXC), ("us", 128, MXS), ("uq2", 128, MXC), ("us2", 128, MXS),
         ("vq", 128, MXC), ("vs", 128, MXS), ("wq", 512, MXC), ("wsc", 512, MXS), ("qx", C, MXC), ("sx", C, MXS),
         ("z", 4 * C, BF), ("h", 4 * C, F32), ("yb", C, F32), ("lof", C, F32),
-        ("cta", 32, I32), ("ctb", 128, F32), ("cto", 128, U16), ("tab", 2048, BF),
+        ("cta", 32, I32), ("ctb", 128, F32), ("cto", 128, U16), ("tab", 2048, BF), ("cfo", 16, U16), ("own", 256, BF),
         ("pint", 2, I32), ("pi2", 4, I32), ("pf", 4, F32), ("kcol", 2, F32), ("uri", 8, I32), ("ur2", 8, I32), ("url", 8, U16),
         ("n16", 192, BF), ("diag", 192, BF), ("m16", 48, BF), ("io32", 32, BF), ("io320", C, F32), ("zz", 192, BF),
         ("fl", 96, BF), ("flm", 96, BF), ("flw", 96, BF), ("dwr", 192, BF), ("lst", 10, U16), ("ul", 8, U16),
@@ -38,13 +38,16 @@ for _n, _c, _d in (
         ("la", 16, F32), ("dd", TO + 32, F32), ("at", 64, F32), ("x4", 80, F32), ("offz", 80, U16),
         ("md", 20, F32), ("lp", 32, F32), ("lt", 64, F32), ("lsw", 32, F32), ("offg", 20, U16), ("offl", 20, U16)):
     _sb(_n, _c, _d)
-SCRATCH["pss"] = ("psum", [128, 3 * 512], F32)
-SCRATCH["psh"] = ("psum", [128, 5 * 512], F32)
+SCRATCH["ps"] = ("psum", [128, 8 * 512], F32)
 
-RING = {"v": 44, "s": 32, "p": 16, "g": 24}
-NDMA = 20
+CHUNKS = ((0, 128), (128, 320))
+LAYER = CHUNKS
+COPIES = ((0, 0, True), (0, 1, False), (0, 2, True), (0, 3, False), (1, 0, True), (1, 1, False), (1, 2, False), (1, 3, False))
+
+RING = {"v": 44, "s": 32, "p": 20, "g": 20}
+NDMA = 18
 SEMAPHORES = ([q + str(k) for q in RING for k in range(RING[q])] + ["d%d" % k for k in range(NDMA)]
-              + ["arr%d" % t for t in range(R)] + ["sent"])
+              + ["arr%d_%d" % (t, k) for t in range(R) for k in range(len(CHUNKS))] + ["sent"])
 
 
 def A(name, c0=None, c1=None, st=1, p0=0, p1=128, ps=1):
@@ -71,10 +74,10 @@ def _meet(a, b):
 
 
 def rank_program(g, core, T, topo):
+    n = len(T.cores)
     rank = T.rank_of(core)
     if rank is None:
         return
-    n = len(T.cores)
     ops = []
     eng = {"v": g.vector, "s": g.scalar, "p": g.tensor, "g": g, "y": g.sync}
     add, mult, sub = AluOpType.add, AluOpType.mult, AluOpType.subtract
@@ -156,15 +159,16 @@ def rank_program(g, core, T, topo):
     def dma(q, o, i, last=False):
         op(q, lambda: eng[q].dma_start(ap(o), ap(i)), [o], [i], kind="dma", last=last)
 
-    def send(t, pairs):
-        dst = T.cores[(rank + 1 + t) % n]
+    def send(t, k):
+        c0, c1 = CHUNKS[k]
+        dst, src = T.cores[(rank + 1 + t) % n], T.cores[(rank - 1 - t) % n]
         rid, pid, _ = topo.addr(dst)
-        mask = topo.mask(core, dst)
+        sem = "arr%d_%d" % (t, k)
+        pairs = [(("b", A("lq%d" % t, c0, c1)), ("b", A("qz%d" % t, c0, c1))), (A("ls%d" % t, c0, c1), A("sz%d" % t, c0, c1))]
         for o, i in pairs:
-            op("g", lambda o=o, i=i: g.remote_dma(ap(o), ap(i), T.sem["arr%d" % t], T.sem.sent, pid, rid, mask), [], [i],
+            op("g", lambda o=o, i=i: g.remote_dma(ap(o), ap(i), T.sem[sem], T.sem.sent, pid, rid, topo.mask(core, dst)), [], [i],
                kind="send", count=len(topo.engines(core, dst)))
-        src = T.cores[(rank - 1 - t) % n]
-        op("none", None, [o for o, i in pairs], [], kind="land", sem="arr%d" % t, val=len(pairs) * len(topo.engines(src, core)))
+        op("none", None, [o for o, i in pairs], [], kind="land", sem=sem, val=len(pairs) * len(topo.engines(src, core)))
 
     dma("y", A("cta", 0, 16), A("ct", 0, 16))
     dma("s", A("cta", 16, 32, p0=0, p1=112), A("ct", 0, 16, p0=16, p1=128))
@@ -180,18 +184,23 @@ def rank_program(g, core, T, topo):
     fill(A("fl"), 0.0)
     fill(A("zz"), 0.0)
     iota(A("pint", 0, 1), [[0, 1]], 0, 1)
+    iota(A("bt", 0, 8), [[3, 4], [0, 2]], TO)
+    iota(A("bt", 8, 12), [[3, 2], [0, 2]], TO + 7)
+    iota(A("bt", 12, 20), [[3, 4], [0, 2]], TO + 2)
     iota(A("uri"), [[16, 8]], 143, -1)
     iota(A("fl", 32, 72), [[32, 4], [16, 2], [1, 5]])
     iota(A("fl", 72, 82), [[-112, 2], [1, 5]], 112)
     iota(A("fl", 0, 12), [[50, 3], [10, 4]], 8)
     iota(A("fl", 12, 15), [[50, 3]], 48)
     iota(A("fl", 16, 28), [[20, 2], [50, 3], [10, 2]], 8)
-    iota(A("bt", 0, 8), [[3, 4], [0, 2]], TO)
-    iota(A("bt", 8, 12), [[3, 2], [0, 2]], TO + 7)
-    iota(A("bt", 12, 20), [[3, 4], [0, 2]], TO + 2)
-    iota(A("ht"), [[0, 10], [1, 2]])
     iota(A("io32"), [[1, 32]], -16)
     iota(A("ji"), [[1, 4], [64, 20]], 0, 4)
+    iota(A("dd"), [[0, TO + 32]])
+    iota(A("d03"), [[0, 96]], 1)
+    iota(A("lp"), [[0, 32]])
+    iota(A("d03", 0, 96, 32), [[0, 3]])
+    const(A("ht", 0, 20, 2), 0)
+    const(A("ht", 1, 20, 2), 1)
     fill(A("dwr"), 1.0)
     fill(A("ul"), 0)
     ts(A("pi2", 0, 1), A("pint", 0, 1), 15, AluOpType.bitwise_and)
@@ -202,72 +211,69 @@ def rank_program(g, core, T, topo):
     copy(A("pf", 0, 3), A("pi2", 0, 3))
     ts(A("ur2"), A("uri"), 112, AluOpType.bitwise_and)
     ts(A("diag"), A("n16"), icol, AluOpType.is_equal)
+    ts(A("f2"), A("bt"), ecol, add, float(-2 * TO), add)
+    ts(A("f1"), A("ht"), ecol, AluOpType.is_equal)
     ts(A("url"), A("ur2"), icol, add)
-    fill(A("thr"), 0.0)
-    fill(A("dd"), 0.0)
-    fill(A("thr", 4, 50, 10), 1e29)
-    fill(A("thr", 9, 50, 10), -1e29)
-    fill(A("lp"), 0.0)
+    tt(A("f3"), A("f1"), A("f2"), mult)
+    tt(A("f4"), A("f3"), A("bt"), add)
+    for e in range(4):
+        tt(A("fm2", 20 * e, 20 * e + 20), A("f4"), A("diag", 20 * e, 20 * e + 20), mult)
     tt(A("flm"), A("fl"), A("diag", 0, 96), mult)
+    scan(A("fw2"), A("dwr", 0, 80), A("fm2"))
     scan(A("flw"), A("dwr", 0, 96), A("flm"))
+    copy(A("lst", 0, 5), A("fw2", 15, 80, 16))
     copy(A("ul", 0, 4), A("flw", 47, 96, 16))
     copy(A("lst", 6, 10, 2), A("flw", 15, 32, 16))
     const(A("hd0"), 2)
     const(A("d1t"), 1)
-    const(A("d03"), 1)
+    const(A("thr"), 0)
     const(A("hd0", 4, 150, 10), 1)
     const(A("hd0", 9, 150, 10), 0)
     for k, slot in ((0, 0), (2, 2), (3, 3), (4, 7)):
         const(A("hd0", 10 * k, 150, 50), 2 * slot)
     const(A("d1t", 0, 192, 32), 0)
     const(A("d1t", 16, 192, 32), 16)
-    const(A("d03", 0, 96, 32), 0)
+    const(A("thr", 4, 50, 10), 1e29)
+    const(A("thr", 9, 50, 10), -1e29)
     act(A("kcol", 0, 1, p0=0, p1=64), A("pf", 1, 2, p0=0, p1=64), scale=-1088.0)
     act(Qd("kcol", 3, 0, 1), Qd("pf", 3, 1, 2), scale=-64.0)
     act(Qd("kcol", 2, 0, 1), Qd("pf", 2, 2, 3), scale=-1088.0, bias=768.0)
     act(A("m16"), A("diag", 0, 48), scale=16.0)
-    dma("g", ("b", A("wq")), A("wc", 0, 2048))
-    dma("g", A("wsc"), A("ws", 0, 512))
-    dma("g", A("vb"), A("v", 0, 512))
-
-    ts(A("f1"), A("ht"), ecol, AluOpType.is_equal)
-    ts(A("f2"), A("bt"), ecol, add, float(-2 * TO), add)
-    tt(A("f3"), A("f1"), A("f2"), mult)
-    tt(A("f4"), A("f3"), A("bt"), add)
-    for e in range(4):
-        tt(A("fm2", 20 * e, 20 * e + 20), A("f4"), A("diag", 20 * e, 20 * e + 20), mult)
-    scan(A("fw2"), A("dwr", 0, 80), A("fm2"))
-    copy(A("lst", 0, 5), A("fw2", 15, 80, 16))
     act(A("j4"), A("ji"), bias=A("kcol", 0, 1))
+    dma("y", ("b", A("wq")), A("wc", 0, 2048))
+    dma("y", A("wsc"), A("ws", 0, 512))
 
+    copy(A("cfo"), A("cta", 0, 16))
+    act(A("own"), ind(A("io32", 16, 32), A("cfo")))
+    for q in (2, 3):
+        o, i = A("tab", 512 * q, 512 * q + 256), A("own", 0, 256, p0=32 * q, p1=32 * q + 1)
+        op("g", lambda o=o, i=i: g.partition_broadcast(ap(o), ap(i), 128), [o], [i])
+    dma("g", A("vb"), A("v", 0, 512))
     copy(A("ctb", 0, 32), A("cta"))
     for q in range(4):
-        if q < 2:
-            copy(Qd("ctb", q, 32, 64), Qd("cta", q + 1, 0, 32))
-        else:
-            act(Qd("ctb", q, 32, 64), Qd("ctb", (q + 1) % 4, 0, 32))
+        copy(Qd("ctb", q, 32, 64), Qd("cta", (q + 1) % 4, 0, 32))
     copy(A("ctb", 64, 128, p0=0, p1=64), A("ctb", 0, 64, p0=64, p1=128))
-    act(A("ctb", 64, 128, p0=64, p1=128), A("ctb", 0, 64, p0=0, p1=64))
+    copy(A("ctb", 64, 128, p0=64, p1=128), A("ctb", 0, 64, p0=0, p1=64))
     copy(A("cto"), ind(A("ctb"), A("url")))
     quant(A("uq"), A("us"), A("ub"))
     act(A("tab", 0, 256), ind(A("io32", 0, 16), A("cto", 0, 16)))
     act(A("tab", 256, 1024), ind(A("io32", 16, 32), A("cto", 16, 64)))
     op("v", lambda: g.vector.tensor_copy(ap(("w", A("uq2"))), ap(("indw", A("uq"), A("ul")))), [A("uq2")], [A("uq"), A("ul")])
     copy(A("us2"), ind(A("us"), A("ul")))
-    act(A("tab", 1024, 1536), ind(A("io32", 16, 32), A("cto", 64, 96)))
+    act(A("tab", 1280, 1536), ind(A("io32", 16, 32), A("cto", 80, 96)))
 
     for t in range(R):
         X, XN = "x%d" % t, "x%d" % (t + 1)
         quant(A("qx", 0, WIN[2]), A("sx", 0, WIN[2]), A(X, 0, 4 * WIN[2]))
         quant(A("qx", WIN[2], C), A("sx", WIN[2], C), A(X, 4 * WIN[2], 4 * C))
         for m in range(3):
-            mm(A("pss", 512 * m, 512 * m + 128), A("qx", WIN[m], WIN[m] + 128), A("sx", WIN[m], WIN[m] + 128), A("uq2"), A("us2"))
+            mm(A("ps", 512 * m, 512 * m + 128), A("qx", WIN[m], WIN[m] + 128), A("sx", WIN[m], WIN[m] + 128), A("uq2"), A("us2"))
         for m in range(3):
-            tt(A("sg", 50 * m, 50 * m + 50), A("pss", 512 * m, 512 * m + 50), A("thr"), AluOpType.is_gt)
+            tt(A("sg", 50 * m, 50 * m + 50), A("ps", 512 * m, 512 * m + 50), A("thr"), AluOpType.is_gt)
         scan(A("sc0"), A("hd0"), A("sg"))
         copy(A("off1"), ind(A("sc0"), A("lst", 6, 7)))
         if t == 0:
-            copy(A("tab", 1536, 2048), ind(A("io32", 16, 32), A("cto", 96, 128)))
+            copy(A("tab", 1792, 2048), ind(A("io32", 16, 32), A("cto", 112, 128)))
         act(A("la"), ind(A("sc0"), A("lst", 8, 9)), scale=4.0)
         for a in range(2):
             for q in range(4):
@@ -294,13 +300,12 @@ def rank_program(g, core, T, topo):
         turn(A("dd", TO, TO + 32), A("at", 16, 48))
         tt(A("x4"), ind(A("dd"), A("lst", 0, 5)), A("j4"), add)
         copy(A("offz"), A("x4"))
-        for e in range(2):
-            act(A("z", e, 4 * C, 4), ind(A(X), A("offz", 20 * e, 20 * e + 20)))
-        for e in range(2, 4):
-            copy(A("z", e, 4 * C, 4), ind(A(X), A("offz", 20 * e, 20 * e + 20)))
         qz, sz, lq, ls = "qz%d" % t, "sz%d" % t, "lq%d" % t, "ls%d" % t
-        quant(A(qz), A(sz), A("z"))
-        send(t, [(("b", A(lq)), ("b", A(qz))), (A(ls), A(sz))])
+        for k, (c0, c1) in enumerate(CHUNKS):
+            for e in range(4):
+                (act if e < 2 else copy)(A("z", 4 * c0 + e, 4 * c1, 4), ind(A(X), A("offz", 20 * e + c0 // 16, 20 * e + c1 // 16)))
+            quant(A(qz, c0, c1), A(sz, c0, c1), A("z", 4 * c0, 4 * c1))
+            send(t, k)
         ts(A("md"), A("x4", 0, 20), float(4 * C), AluOpType.is_ge, float(-4 * C), mult)
         tt(A("lp", 0, 20), A("x4", 0, 20), A("md"), add)
         turn(A("lt", 0, 32), A("lp"))
@@ -314,15 +319,17 @@ def rank_program(g, core, T, topo):
             ts(A("offl"), A("lp", 0, 20), 0.25, mult)
             act(A("lof"), ind(A("io320"), A("offl")))
             dma("y", A("lo", 0, C, p0=0, p1=8), A("lof", 0, C, ps=16), last=True)
-        hc = C // 2
-        mm(A("psh", 0, hc), A("wq", 0, 128), A("wsc", 0, 128), A(lq, 0, hc), A(ls, 0, hc))
-        mm(A("psh", 2048, 2048 + hc), A("wq", 0, 128), A("wsc", 0, 128), A(lq, hc, C), A(ls, hc, C))
-        for b in range(1, 4):
-            mm(A("psh", 512 * b, 512 * b + C), A("wq", 128 * b, 128 * b + 128), A("wsc", 128 * b, 128 * b + 128), A(lq), A(ls))
-        act(A("h", 0, hc), A("psh", 0, hc), scale=0.03125)
-        ts(A("h", hc, C), A("psh", 2048, 2048 + hc), 0.03125, mult)
-        for b in range(1, 4):
-            act(A("h", C * b, C * b + C), A("psh", 512 * b, 512 * b + C), scale=0.03125)
+        for k, b, on_v in COPIES:
+            c0, c1 = LAYER[k]
+            mm(A("ps", 512 * (4 * k + b), 512 * (4 * k + b) + c1 - c0), A("wq", 128 * b, 128 * b + 128), A("wsc", 128 * b, 128 * b + 128),
+               A(lq, c0, c1), A(ls, c0, c1))
+        for k, b, on_v in COPIES:
+            c0, c1 = LAYER[k]
+            o, i = A("h", C * b + c0, C * b + c1), A("ps", 512 * (4 * k + b), 512 * (4 * k + b) + c1 - c0)
+            if on_v:
+                ts(o, i, 0.03125, mult)
+            else:
+                act(o, i, scale=0.03125)
         for b in range(4):
             tt(A(XN, b, 4 * C, 4), ind(A("h", C * b, C * b + C), A("offg")), A(X, b, 4 * C, 4), add)
         if t < R - 1:
@@ -332,13 +339,13 @@ def rank_program(g, core, T, topo):
     cut = WIN[2]
     quant(A("qx", 0, cut), A("sx", 0, cut), A("x%d" % R, 0, 4 * cut))
     quant(A("qx", cut, C), A("sx", cut, C), A("x%d" % R, 4 * cut, 4 * C))
-    mm(A("pss", 0, cut), A("vq"), A("vs"), A("qx", 0, cut), A("sx", 0, cut))
-    mm(A("pss", 512, 512 + C - cut), A("vq"), A("vs"), A("qx", cut, C), A("sx", cut, C))
+    mm(A("ps", 0, cut), A("vq"), A("vs"), A("qx", 0, cut), A("sx", 0, cut))
+    mm(A("ps", 512, 512 + C - cut), A("vq"), A("vs"), A("qx", cut, C), A("sx", cut, C))
     dma("y", A("oc", 0, 4 * C), ("b", A("qx")), last=True)
     for k in range(4):
         dma("s" if k < 3 else "g", A("osc", 0, C, p0=4 * k, p1=4 * k + 4), A("sx", 0, C, p0=32 * k, p1=32 * k + 4), last=True)
-    copy(A("yb", 0, cut), A("pss", 0, cut))
-    copy(A("yb", cut, C), A("pss", 512, 512 + C - cut))
+    copy(A("yb", 0, cut), A("ps", 0, cut))
+    copy(A("yb", cut, C), A("ps", 512, 512 + C - cut))
     dma("y", A("y", 0, C), A("yb"), last=True)
 
     known = {}

from concourse.mybir import dt, AluOpType, ActivationFunctionType

C = 320
R = 3
EXT = 256
WIN = (0, 64, 192)
TO = 72
F32, BF, I32, U16 = "float32", "bfloat16", "int32", "uint16"
MXC, MXS = "float8_e4m3fn_x4", "uint8"

SCRATCH = {}


def _sb(name, cols, dtype):
    SCRATCH[name] = ("sbuf", [128, cols], dtype)


for _t in range(R):
    _sb("x%d" % _t, 4 * (C + EXT), BF)
    _sb("qz%d" % _t, C, MXC)
    _sb("sz%d" % _t, C, MXS)
    _sb("lq%d" % _t, C, MXC)
    _sb("ls%d" % _t, C, MXS)
_sb("x%d" % R, 4 * C, BF)
for _n, _c, _d in (
        ("ub", 512, BF), ("vb", 512, BF), ("uq", 128, MXC), ("us", 128, MXS), ("uq2", 128, MXC), ("us2", 128, MXS),
        ("vq", 128, MXC), ("vs", 128, MXS), ("wq", 512, MXC), ("wsc", 512, MXS), ("qx", C, MXC), ("sx", C, MXS),
        ("z", 4 * C, BF), ("h", 4 * C, F32), ("yb", C, F32), ("lof", C, F32),
        ("cta", 32, I32), ("ctb", 128, F32), ("cto", 128, U16), ("tab", 2048, BF), ("cfo", 16, U16), ("own", 256, BF),
        ("pint", 2, I32), ("pi2", 4, I32), ("pf", 4, F32), ("kcol", 2, F32), ("uri", 8, I32), ("ur2", 8, I32), ("url", 8, U16),
        ("n16", 192, BF), ("diag", 192, BF), ("m16", 48, BF), ("io32", 32, BF), ("io320", C, F32), ("zz", 192, BF),
        ("fl", 96, BF), ("flm", 96, BF), ("flw", 96, BF), ("dwr", 192, BF), ("lst", 10, U16), ("ul", 8, U16),
        ("fm2", 80, BF), ("fw2", 80, BF),
        ("bt", 20, F32), ("ht", 20, F32), ("f1", 20, F32), ("f2", 20, F32), ("f3", 20, F32), ("f4", 20, F32),
        ("ji", 80, F32), ("j4", 80, F32), ("hd0", 150, F32), ("thr", 50, F32), ("d1t", 192, BF), ("d03", 96, BF),
        ("sg", 150, F32), ("sc0", 150, F32), ("off1", 16, U16), ("g1", 192, BF), ("sc1", 192, BF), ("off2", 6, U16),
        ("g2", 96, BF), ("sc2", 96, BF), ("off3", 4, U16), ("g3", 96, BF), ("sc3", 96, BF),
        ("la", 16, F32), ("dd", TO + 32, F32), ("at", 64, F32), ("x4", 80, F32), ("offz", 80, U16),
        ("md", 20, F32), ("lp", 32, F32), ("lt", 64, F32), ("lsw", 32, F32), ("offg", 20, U16), ("offl", 20, U16)):
    _sb(_n, _c, _d)
SCRATCH["ps"] = ("psum", [128, 8 * 512], F32)

CHUNKS = ((0, 128), (128, 320))
LAYER = CHUNKS
COPIES = ((0, 0, True), (0, 1, False), (0, 2, True), (0, 3, False), (1, 0, True), (1, 1, False), (1, 2, False), (1, 3, False))

RING = {"v": 44, "s": 32, "p": 20, "g": 20}
NDMA = 18
SEMAPHORES = ([q + str(k) for q in RING for k in range(RING[q])] + ["d%d" % k for k in range(NDMA)]
              + ["arr%d_%d" % (t, k) for t in range(R) for k in range(len(CHUNKS))] + ["sent"])


def A(name, c0=None, c1=None, st=1, p0=0, p1=128, ps=1):
    if c0 is None:
        c0, c1 = 0, SCRATCH[name][1][1]
    return (name, p0, p1, ps, c0, c1, st)


def Qd(name, q, c0, c1, st=1):
    return A(name, c0, c1, st, 32 * q, 32 * q + 32)


def _foot(a):
    name, p0, p1, ps, c0, c1, st = a
    if name not in SCRATCH:
        return None
    if SCRATCH[name][0] == "psum":
        return (name, 0, 128, frozenset(range(c0 // 512, (c1 - 1) // 512 + 1)), True)
    return (name, p0, p1, frozenset(range(c0, c1, st)), False)


def _meet(a, b):
    return a[0] == b[0] and a[1] < b[2] and b[1] < a[2] and not a[3].isdisjoint(b[3])


def rank_program(g, core, T, topo):
    n = len(T.cores)
    rank = T.rank_of(core)
    if rank is None:
        return
    ops = []
    eng = {"v": g.vector, "s": g.scalar, "p": g.tensor, "g": g, "y": g.sync}
    add, mult, sub = AluOpType.add, AluOpType.mult, AluOpType.subtract
    COPY, IDENT = ActivationFunctionType.Copy, ActivationFunctionType.Identity

    def ap(a):
        if not isinstance(a, tuple):
            return a
        if a[0] == "ind":
            return ap(a[1]).indirect(ap(a[2]))
        if a[0] == "indw":
            return ap(a[1]).bitcast(dt.uint32).indirect(ap(a[2]))
        if a[0] == "w":
            return ap(a[1]).bitcast(dt.uint32)
        if a[0] == "b":
            return ap(a[1]).bitcast(dt.uint8)
        name, p0, p1, ps, c0, c1, st = a
        return T[name][slice(p0, p1, ps) if ps > 1 else slice(p0, p1), slice(c0, c1, st) if st > 1 else slice(c0, c1)]

    def feet(args):
        out = []
        for a in args:
            if isinstance(a, tuple):
                if a[0] in ("ind", "indw", "w", "b"):
                    out += feet(a[1:])
                elif _foot(a) is not None:
                    out.append(_foot(a))
        return out

    def op(q, call, outs, ins, kind="c", **more):
        w, r = feet(outs), feet(ins)
        w += [f for f in r if f[4]]
        ops.append(dict(q=q, call=call, w=w, r=r, kind=kind, **more))

    def ind(win, off):
        return ("ind", win, off)

    def copy(o, i):
        op("v", lambda: g.vector.tensor_copy(ap(o), ap(i)), [o], [i])

    def tt(o, a, b, f):
        op("v", lambda: g.vector.tensor_tensor(ap(o), ap(a), ap(b), f), [o], [a, b])

    def ts(o, a, s1, f1, s2=None, f2=None):
        if f2 is None:
            op("v", lambda: g.vector.tensor_scalar(ap(o), ap(a), ap(s1), None, f1), [o], [a, s1])
        else:
            op("v", lambda: g.vector.tensor_scalar(ap(o), ap(a), ap(s1), ap(s2), f1, f2), [o], [a, s1, s2])

    def scan(o, d0, d1):
        op("v", lambda: g.vector.tensor_tensor_scan(ap(o), ap(d0), ap(d1), 0.0, mult, add), [o], [d0, d1])

    def fill(o, c):
        op("v", lambda: g.vector.memset(ap(o), c), [o], [])

    def turn(o, i):
        op("v", lambda: g.vector.transpose(ap(o), ap(i)), [o], [i])

    def quant(q, s, i):
        op("v", lambda: g.vector.quantize_mx(ap(q), ap(s), ap(i)), [q, s], [i])

    def act(o, i, scale=None, bias=None):
        if bias is not None:
            op("s", lambda: g.scalar.activation(ap(o), ap(i), IDENT, bias=ap(bias), scale=1.0 if scale is None else scale), [o], [i, bias])
        elif scale is not None:
            op("s", lambda: g.scalar.activation(ap(o), ap(i), COPY, scale=scale), [o], [i])
        else:
            op("s", lambda: g.scalar.activation(ap(o), ap(i), COPY), [o], [i])

    def mm(o, lq, ls, rq, rs):
        op("p", lambda: g.tensor.matmul_mx(ap(o), ap(lq), ap(ls), ap(rq), ap(rs), True, True), [o], [lq, ls, rq, rs])

    def iota(o, pattern, base=0, cm=0):
        if SCRATCH[o[0]][2] == I32:
            op("g", lambda: g.iota(ap(o), pattern, base, cm), [o], [])
        else:
            op("g", lambda: g.iota(ap(o), pattern, base, cm, allow_small_or_imprecise_dtypes=True), [o], [])

    def dma(q, o, i, last=False):
        op(q, lambda: eng[q].dma_start(ap(o), ap(i)), [o], [i], kind="dma", last=last)

    def send(t, k):
        c0, c1 = CHUNKS[k]
        dst, src = T.cores[(rank + 1 + t) % n], T.cores[(rank - 1 - t) % n]
        rid, pid, _ = topo.addr(dst)
        sem = "arr%d_%d" % (t, k)
        pairs = [(("b", A("lq%d" % t, c0, c1)), ("b", A("qz%d" % t, c0, c1))), (A("ls%d" % t, c0, c1), A("sz%d" % t, c0, c1))]
        for o, i in pairs:
            op("g", lambda o=o, i=i: g.remote_dma(ap(o), ap(i), T.sem[sem], T.sem.sent, pid, rid, topo.mask(core, dst)), [], [i],
               kind="send", count=len(topo.engines(core, dst)))
        op("none", None, [o for o, i in pairs], [], kind="land", sem=sem, val=len(pairs) * len(topo.engines(src, core)))

    dma("y", A("cta", 0, 16), A("ct", 0, 16))
    dma("s", A("cta", 16, 32, p0=0, p1=112), A("ct", 0, 16, p0=16, p1=128))
    dma("y", A("cta", 16, 32, p0=112, p1=128), A("ct", 0, 16, p0=0, p1=16))
    dma("s", A("ub"), A("u", 0, 512))
    dma("y", A("x0", 0, 4 * C), A("x", 0, 4 * C))
    dma("y", A("x0", 4 * C, 4 * (C + EXT)), A("x", 0, 4 * EXT))

    def const(o, c):
        act(o, A("zz", 0, len(range(o[4], o[5], o[6]))), bias=float(c))

    icol, gcol, ecol = A("pf", 0, 1), A("pf", 1, 2), A("pf", 2, 3)
    fill(A("fl"), 0.0)
    fill(A("zz"), 0.0)
    iota(A("pint", 0, 1), [[0, 1]], 0, 1)
    iota(A("bt", 0, 8), [[3, 4], [0, 2]], TO)
    iota(A("bt", 8, 12), [[3, 2], [0, 2]], TO + 7)
    iota(A("bt", 12, 20), [[3, 4], [0, 2]], TO + 2)
    iota(A("uri"), [[16, 8]], 143, -1)
    iota(A("fl", 32, 72), [[32, 4], [16, 2], [1, 5]])
    iota(A("fl", 72, 82), [[-112, 2], [1, 5]], 112)
    iota(A("fl", 0, 12), [[50, 3], [10, 4]], 8)
    iota(A("fl", 12, 15), [[50, 3]], 48)
    iota(A("fl", 16, 28), [[20, 2], [50, 3], [10, 2]], 8)
    iota(A("io32"), [[1, 32]], -16)
    iota(A("ji"), [[1, 4], [64, 20]], 0, 4)
    iota(A("dd"), [[0, TO + 32]])
    iota(A("d03"), [[0, 96]], 1)
    iota(A("lp"), [[0, 32]])
    iota(A("d03", 0, 96, 32), [[0, 3]])
    const(A("ht", 0, 20, 2), 0)
    const(A("ht", 1, 20, 2), 1)
    fill(A("dwr"), 1.0)
    fill(A("ul"), 0)
    ts(A("pi2", 0, 1), A("pint", 0, 1), 15, AluOpType.bitwise_and)
    fill(A("dwr", 0, 192, 16), 0.0)
    ts(A("pi2", 1, 2), A("pint", 0, 1), 4, AluOpType.arith_shift_right)
    ts(A("pi2", 2, 3), A("pint", 0, 1), 4, AluOpType.arith_shift_right, 1, AluOpType.bitwise_and)
    scan(A("n16"), A("dwr"), A("dwr"))
    copy(A("pf", 0, 3), A("pi2", 0, 3))
    ts(A("ur2"), A("uri"), 112, AluOpType.bitwise_and)
    ts(A("diag"), A("n16"), icol, AluOpType.is_equal)
    ts(A("f2"), A("bt"), ecol, add, float(-2 * TO), add)
    ts(A("f1"), A("ht"), ecol, AluOpType.is_equal)
    ts(A("url"), A("ur2"), icol, add)
    tt(A("f3"), A("f1"), A("f2"), mult)
    tt(A("f4"), A("f3"), A("bt"), add)
    for e in range(4):
        tt(A("fm2", 20 * e, 20 * e + 20), A("f4"), A("diag", 20 * e, 20 * e + 20), mult)
    tt(A("flm"), A("fl"), A("diag", 0, 96), mult)
    scan(A("fw2"), A("dwr", 0, 80), A("fm2"))
    scan(A("flw"), A("dwr", 0, 96), A("flm"))
    copy(A("lst", 0, 5), A("fw2", 15, 80, 16))
    copy(A("ul", 0, 4), A("flw", 47, 96, 16))
    copy(A("lst", 6, 10, 2), A("flw", 15, 32, 16))
    const(A("hd0"), 2)
    const(A("d1t"), 1)
    const(A("thr"), 0)
    const(A("hd0", 4, 150, 10), 1)
    const(A("hd0", 9, 150, 10), 0)
    for k, slot in ((0, 0), (2, 2), (3, 3), (4, 7)):
        const(A("hd0", 10 * k, 150, 50), 2 * slot)
    const(A("d1t", 0, 192, 32), 0)
    const(A("d1t", 16, 192, 32), 16)
    const(A("thr", 4, 50, 10), 1e29)
    const(A("thr", 9, 50, 10), -1e29)
    act(A("kcol", 0, 1, p0=0, p1=64), A("pf", 1, 2, p0=0, p1=64), scale=-1088.0)
    act(Qd("kcol", 3, 0, 1), Qd("pf", 3, 1, 2), scale=-64.0)
    act(Qd("kcol", 2, 0, 1), Qd("pf", 2, 2, 3), scale=-1088.0, bias=768.0)
    act(A("m16"), A("diag", 0, 48), scale=16.0)
    act(A("j4"), A("ji"), bias=A("kcol", 0, 1))
    dma("y", ("b", A("wq")), A("wc", 0, 2048))
    dma("y", A("wsc"), A("ws", 0, 512))

    copy(A("cfo"), A("cta", 0, 16))
    act(A("own"), ind(A("io32", 16, 32), A("cfo")))
    for q in (2, 3):
        o, i = A("tab", 512 * q, 512 * q + 256), A("own", 0, 256, p0=32 * q, p1=32 * q + 1)
        op("g", lambda o=o, i=i: g.partition_broadcast(ap(o), ap(i), 128), [o], [i])
    dma("g", A("vb"), A("v", 0, 512))
    copy(A("ctb", 0, 32), A("cta"))
    for q in range(4):
        copy(Qd("ctb", q, 32, 64), Qd("cta", (q + 1) % 4, 0, 32))
    copy(A("ctb", 64, 128, p0=0, p1=64), A("ctb", 0, 64, p0=64, p1=128))
    copy(A("ctb", 64, 128, p0=64, p1=128), A("ctb", 0, 64, p0=0, p1=64))
    copy(A("cto"), ind(A("ctb"), A("url")))
    quant(A("uq"), A("us"), A("ub"))
    act(A("tab", 0, 256), ind(A("io32", 0, 16), A("cto", 0, 16)))
    act(A("tab", 256, 1024), ind(A("io32", 16, 32), A("cto", 16, 64)))
    op("v", lambda: g.vector.tensor_copy(ap(("w", A("uq2"))), ap(("indw", A("uq"), A("ul")))), [A("uq2")], [A("uq"), A("ul")])
    copy(A("us2"), ind(A("us"), A("ul")))
    act(A("tab", 1280, 1536), ind(A("io32", 16, 32), A("cto", 80, 96)))

    for t in range(R):
        X, XN = "x%d" % t, "x%d" % (t + 1)
        quant(A("qx", 0, WIN[2]), A("sx", 0, WIN[2]), A(X, 0, 4 * WIN[2]))
        quant(A("qx", WIN[2], C), A("sx", WIN[2], C), A(X, 4 * WIN[2], 4 * C))
        for m in range(3):
            mm(A("ps", 512 * m, 512 * m + 128), A("qx", WIN[m], WIN[m] + 128), A("sx", WIN[m], WIN[m] + 128), A("uq2"), A("us2"))
        for m in range(3):
            tt(A("sg", 50 * m, 50 * m + 50), A("ps", 512 * m, 512 * m + 50), A("thr"), AluOpType.is_gt)
        scan(A("sc0"), A("hd0"), A("sg"))
        copy(A("off1"), ind(A("sc0"), A("lst", 6, 7)))
        if t == 0:
            copy(A("tab", 1792, 2048), ind(A("io32", 16, 32), A("cto", 112, 128)))
        act(A("la"), ind(A("sc0"), A("lst", 8, 9)), scale=4.0)
        for a in range(2):
            for q in range(4):
                act(Qd("dd", a, 6 * q, 6 * q + 6), Qd("la", q, 6 * a, 6 * a + 6))
        tt(A("g1"), ind(A("tab", 0, 1024), A("off1", 0, 12)), A("diag"), mult)
        scan(A("sc1"), A("d1t"), A("g1"))
        ts(A("off2"), A("sc1", 31, 192, 32), 256.0, add)
        for q in range(4):
            act(Qd("dd", 2, 6 * q, 6 * q + 6), Qd("sc1", q, 31, 192, 32), scale=4.0)
        tt(A("g2"), ind(A("tab", 1024, 1536), A("off2")), A("diag", 0, 96), mult)
        tt(A("g3", 1, 96, 2), ind(A("tab"), A("off1", 12, 15)), A("diag", 0, 48), mult)
        scan(A("sc2"), A("d1t", 0, 96), A("g2"))
        copy(A("off3", 0, 3), A("sc2", 31, 96, 32))
        for q in range(4):
            act(Qd("dd", 3, 6 * q, 6 * q + 6, 2), Qd("sc2", q, 31, 96, 32), scale=4.0)
        tt(A("g3", 0, 96, 2), ind(A("tab", 1536, 1792), A("off3", 0, 3)), A("m16"), mult)
        scan(A("sc3"), A("d03"), A("g3"))
        for q in range(2):
            ts(Qd("dd", 3, 6 * q + 1, 6 * q + 6, 2), Qd("sc3", q, 31, 96, 32), 4.0, mult)
        for q in range(2, 4):
            act(Qd("dd", 3, 6 * q + 1, 6 * q + 6, 2), Qd("sc3", q, 31, 96, 32), scale=4.0)
        turn(A("at", 0, 32), A("dd", 0, 64, 2))
        turn(A("at", 32, 64), A("dd", 1, 65, 2))
        turn(A("dd", TO, TO + 32), A("at", 16, 48))
        tt(A("x4"), ind(A("dd"), A("lst", 0, 5)), A("j4"), add)
        copy(A("offz"), A("x4"))
        qz, sz, lq, ls = "qz%d" % t, "sz%d" % t, "lq%d" % t, "ls%d" % t
        for k, (c0, c1) in enumerate(CHUNKS):
            for e in range(4):
                (act if e < 2 else copy)(A("z", 4 * c0 + e, 4 * c1, 4), ind(A(X), A("offz", 20 * e + c0 // 16, 20 * e + c1 // 16)))
            quant(A(qz, c0, c1), A(sz, c0, c1), A("z", 4 * c0, 4 * c1))
            send(t, k)
        ts(A("md"), A("x4", 0, 20), float(4 * C), AluOpType.is_ge, float(-4 * C), mult)
        tt(A("lp", 0, 20), A("x4", 0, 20), A("md"), add)
        turn(A("lt", 0, 32), A("lp"))
        turn(A("lt", 32, 64), A("lp"))
        turn(A("lsw"), A("lt", 16, 48))
        ts(A("offg"), A("lsw", 0, 20), 0.25, mult)
        if t == 0:
            quant(A("vq"), A("vs"), A("vb"))
            iota(A("io320"), [[1, C]])
        if t == R - 1:
            ts(A("offl"), A("lp", 0, 20), 0.25, mult)
            act(A("lof"), ind(A("io320"), A("offl")))
            dma("y", A("lo", 0, C, p0=0, p1=8), A("lof", 0, C, ps=16), last=True)
        for k, b, on_v in COPIES:
            c0, c1 = LAYER[k]
            mm(A("ps", 512 * (4 * k + b), 512 * (4 * k + b) + c1 - c0), A("wq", 128 * b, 128 * b + 128), A("wsc", 128 * b, 128 * b + 128),
               A(lq, c0, c1), A(ls, c0, c1))
        for k, b, on_v in COPIES:
            c0, c1 = LAYER[k]
            o, i = A("h", C * b + c0, C * b + c1), A("ps", 512 * (4 * k + b), 512 * (4 * k + b) + c1 - c0)
            if on_v:
                ts(o, i, 0.03125, mult)
            else:
                act(o, i, scale=0.03125)
        for b in range(4):
            tt(A(XN, b, 4 * C, 4), ind(A("h", C * b, C * b + C), A("offg")), A(X, b, 4 * C, 4), add)
        if t < R - 1:
            for b in range(4):
                act(A(XN, 4 * C + b, 4 * (C + EXT), 4), A(XN, b, 4 * EXT, 4))

    cut = WIN[2]
    quant(A("qx", 0, cut), A("sx", 0, cut), A("x%d" % R, 0, 4 * cut))
    quant(A("qx", cut, C), A("sx", cut, C), A("x%d" % R, 4 * cut, 4 * C))
    mm(A("ps", 0, cut), A("vq"), A("vs"), A("qx", 0, cut), A("sx", 0, cut))
    mm(A("ps", 512, 512 + C - cut), A("vq"), A("vs"), A("qx", cut, C), A("sx", cut, C))
    dma("y", A("oc", 0, 4 * C), ("b", A("qx")), last=True)
    for k in range(4):
        dma("s" if k < 3 else "g", A("osc", 0, C, p0=4 * k, p1=4 * k + 4), A("sx", 0, C, p0=32 * k, p1=32 * k + 4), last=True)
    copy(A("yb", 0, cut), A("ps", 0, cut))
    copy(A("yb", cut, C), A("ps", 512, 512 + C - cut))
    dma("y", A("y", 0, C), A("yb"), last=True)

    known = {}
    for k, o in enumerate(ops):
        o["waits"] = []
        seen = known.setdefault(o["q"], set())
        if o["kind"] != "land":
            for j in range(k - 1, -1, -1):
                e = ops[j]
                if j in seen or (o["q"] == "p" and e["q"] == "p"):
                    continue
                if (any(_meet(a, b) for a in o["r"] + o["w"] for b in e["w"]) or any(_meet(a, b) for a in o["w"] for b in e["r"])):
                    o["waits"].append(j)
                    e["need"] = True
                    seen.add(j)
                    seen.update(e["seen"])
        o["seen"] = set(seen)
    level, turnq, nd = {}, {}, 0
    for o in ops:
        if o["kind"] == "dma":
            o["sem"], o["val"] = "d%d" % nd, 16
            nd += 1
        elif o["kind"] == "c" and o.get("need"):
            k = turnq.get(o["q"], 0)
            turnq[o["q"]] = k + 1
            o["sem"] = o["q"] + str(k % RING[o["q"]])
            level[o["sem"]] = level.get(o["sem"], 0) + 1
            o["val"] = level[o["sem"]]
    sent = 0
    for o in ops:
        if o["kind"] == "land":
            continue
        for j in o["waits"]:
            eng[o["q"]].wait_ge(T.sem[ops[j]["sem"]], ops[j]["val"])
        ins = o["call"]()
        if o["kind"] == "send":
            sent += o["count"]
        elif o["kind"] == "dma":
            ins.then_inc(T.sem[o["sem"]], 16)
        elif o.get("need"):
            ins.then_inc(T.sem[o["sem"]], 1)
    g.wait_ge(T.sem.sent, sent)
    for o in ops:
        if o["kind"] == "dma" and o["last"]:
            eng[o["q"]].wait_ge(T.sem[o["sem"]], 16)
